import numpy as np
import ml_dtypes


def mxq(x, axis, fmt="e4m3"):
    dtype, down = {"e4m3": (ml_dtypes.float8_e4m3fn, 7), "e5m2": (ml_dtypes.float8_e5m2, 14)}[fmt]
    v = np.moveaxis(np.asarray(x, np.float32).astype(ml_dtypes.bfloat16).astype(np.float64), axis, -1)
    blocks = v.reshape(v.shape[:-1] + (-1, 32))
    amax = np.abs(blocks).max(-1, keepdims=True)
    byte = np.maximum(np.where(amax > 0, np.frexp(amax)[1] - 1 + 127, 0) - down, 1)
    scale = np.exp2(byte - 127.0)
    codes = (blocks / scale).astype(np.float32).astype(dtype).astype(np.float64)
    return np.moveaxis((codes * scale).reshape(v.shape), -1, axis)


WIDE = False


def mx_kscale(k):
    if not WIDE:
        return np.ones(k)
    levels = np.array([10, -10, 5, -5, 0])
    if k % 512:
        return np.exp2(np.random.permutation(np.resize(levels, k // 32))).repeat(32)
    a = np.empty((k // 512, 16))
    for p in range(k // 512):
        a[p, :8] = np.random.permutation(np.resize(levels, 8))
        for g in range(8):
            far = levels[np.abs(levels - a[p, g]) >= 10]
            a[p, g + 8] = far[np.random.randint(len(far))]
    return np.exp2(a.ravel()).repeat(32)


BF16 = ml_dtypes.bfloat16


def bf(x):
    return np.asarray(x, np.float32).astype(BF16)


def f64(x):
    return np.asarray(x).astype(np.float64)


E2M1 = np.array([0.0, 0.5, 1.0, 1.5, 2.0, 3.0, 4.0, 6.0, -0.0, -0.5, -1.0, -1.5, -2.0, -3.0, -4.0, -6.0])


def pack_weight(w, fmt):
    k, n = w.shape
    w = f64(bf(w)).reshape(k // 32, 32, n)
    amax = np.abs(w).max(1)
    if fmt == "e4m3":
        byte = np.frexp(amax)[1] - 1 + 127 - 7
    else:
        mant, ex = np.frexp(amax / 6.0)
        byte = np.where(mant > 0.5, ex, ex - 1) + 127
    byte = np.clip(np.where(amax > 0, byte, 1), 1, 254)
    scaled = (w * np.exp2(127.0 - byte)[:, None, :]).reshape(k, n).astype(np.float32)
    by_word = np.ascontiguousarray(scaled.reshape(k // 512, 128, 4, n).transpose(0, 1, 3, 2))
    if fmt == "e4m3":
        words = by_word.astype(ml_dtypes.float8_e4m3fn).view(np.uint8)
    else:
        c = by_word.astype(ml_dtypes.float4_e2m1fn).view(np.uint8) & 0xF
        words = c[..., 0::2] | (c[..., 1::2] << 4)
    return np.ascontiguousarray(words), np.ascontiguousarray(byte.astype(np.uint8).reshape(k // 512, 16, n))


def unpack_weight(words, scales, fmt):
    g, p, n, _ = words.shape
    if fmt == "e4m3":
        vals = np.ascontiguousarray(words).view(ml_dtypes.float8_e4m3fn).astype(np.float64)
    else:
        nib = np.empty((g, p, n, 4), np.uint8)
        nib[..., 0::2] = words & 0xF
        nib[..., 1::2] = words >> 4
        vals = E2M1[nib]
    vals = vals * np.repeat(np.exp2(scales.astype(np.float64) - 127.0), 8, axis=1)[..., None]
    return vals.transpose(0, 1, 3, 2).reshape(g * 512, n)
def pack4(w):
    words, scales = pack_weight(w, "e2m1")
    return words.reshape(words.shape[0], 128, -1), scales


def unpack4(words, scales):
    return unpack_weight(words.reshape(words.shape[0], 128, -1, 2), scales, "e2m1")


T, NA, NB, F, V = 1024, 1024, 1536, 1024, 2048


def setup_inputs():
    sa = mx_kscale(NA)
    sb = mx_kscale(NB)
    u = mx_kscale(F)
    pb = np.random.standard_normal((NB, F)) / np.sqrt(NA + NB) / sb[:, None] * u
    load = np.random.standard_normal((F, V)) / np.sqrt(F) / u[:, None]
    pb_words, pb_scales = pack4(pb)
    load_words, load_scales = pack4(load)
    return {"ra": bf(np.random.standard_normal((T, NA)) * sa),
            "pa": bf(np.random.standard_normal((NA, F)) / np.sqrt(NA + NB) / sa[:, None] * u),
            "rb": bf(np.random.standard_normal((T, NB)) * sb),
            "pb_words": pb_words, "pb_scales": pb_scales,
            "shrink": bf(1 + 0.1 * np.random.standard_normal(F)),
            "prior": bf(0.3 * np.random.standard_normal(F) * u),
            "load_words": load_words, "load_scales": load_scales,
            "y": bf(np.random.standard_normal((T, V))),
            "inv_vol": bf(1 + 0.1 * np.random.standard_normal(V))}


def reference(ra, pa, rb, pb_words, pb_scales, shrink, prior, load_words, load_scales, y, inv_vol):
    raw = ((mxq(f64(ra), 1, "e4m3") @ mxq(f64(pa), 0, "e4m3"))
           + (mxq(f64(rb), 1, "e4m3") @ unpack4(pb_words, pb_scales)))
    premia = raw * f64(shrink) + f64(prior)
    fit = mxq(premia, 1, "e4m3") @ unpack4(load_words, load_scales)
    return (f64(y) - fit) * f64(inv_vol)

@@ -1,0 +1,439 @@
+from contextlib import ExitStack
+
+import concourse.mybir as mybir
+from concourse.masks import make_identity
+
+F32 = mybir.dt.float32
+BF16 = mybir.dt.bfloat16
+I32 = mybir.dt.int32
+U32 = mybir.dt.uint32
+U8 = mybir.dt.uint8
+FP8X4 = mybir.dt.float8_e4m3fn_x4
+FP4X4 = mybir.dt.float4_e2m1fn_x4
+ALU = mybir.AluOpType
+ACTF = mybir.ActivationFunctionType
+
+P = 128
+T, NA, NB, F, V = 1024, 1024, 1536, 1024, 2048
+FLOPS = 2 * T * F * (NA + NB) + 2 * T * F * V
+
+HALF = 512
+CA = NA // 512
+CB = NB // 512
+UNITS = [(b, v) for b in range(4) for v in range(4)]
+B_ON_VECTOR = 3
+
+
+def tile_cross_sectional_premia_residuals_s3_kernel(
+    tc, ra, pa, rb, pb_words, pb_scales, shrink, prior, load_words, load_scales, y, inv_vol, out
+):
+    nc = tc.nc
+    with ExitStack() as ctx:
+        keep = ctx.enter_context(tc.tile_pool(name="keep", bufs=1))
+        stage = ctx.enter_context(tc.tile_pool(name="stage", bufs=2))
+        psum = ctx.enter_context(tc.psum_pool(name="psum", bufs=1))
+        ctx.enter_context(tc.manual_schedule())
+
+        def bank(i):
+            return psum.tile([P, 512], F32, name=f"bank{i}", tag=f"bank{i}", bufs=1)
+
+        def kept(shape, dtype, name):
+            return keep.tile(shape, dtype, name=name, tag=name, align_bytes=64)
+
+        ident = kept([P, P], F32, "ident")
+        pb_raw = [kept([P, CB, 1024], U8, f"pb_raw{g}") for g in range(2)]
+        pbs_raw = kept([P, CB, F], U8, "pbs_raw")
+        pbw = [[kept([P, 1024], U8, f"pbw{g}_{c}") for c in range(CB)] for g in range(2)]
+        pbs = [[kept([P, 512], U8, f"pbs{g}_{c}") for c in range(CB)] for g in range(2)]
+        lw = kept([P, 2, 2 * V], U8, "lw")
+        ls = kept([P, 2, V], U8, "ls")
+        shrink_raw = kept([P, 2, 4], BF16, "shrink_raw")
+        prior_raw = kept([P, 2, 4], BF16, "prior_raw")
+        shrink_f = kept([P, 2, 4], F32, "shrink_f")
+        prior_f = kept([P, 2, 4], F32, "prior_f")
+        warm = kept([P, 1], F32, "warm")
+        iv = kept([P, V], BF16, "iv")
+        xa = [[kept([P, 2, NA], BF16, f"xa{h}{q}") for q in range(2)] for h in range(2)]
+        xb = [[kept([P, 2, NB], BF16, f"xb{h}{q}") for q in range(2)] for h in range(2)]
+        pa_raw = [[kept([P, 4, 512], BF16, f"pa_raw{g}{c}") for c in range(CA)] for g in range(2)]
+        ysb = [[kept([P, 2, V], BF16, f"y{h}{q}") for q in range(2)] for h in range(2)]
+        paw = [[kept([P, 512], U32, f"paw{g}{c}") for c in range(CA)] for g in range(2)]
+        pas = [[kept([P, 512], U8, f"pas{g}{c}") for c in range(CA)] for g in range(2)]
+        xw = [[kept([P, 512], U32, f"xw{h}{c}") for c in range(CA + CB)] for h in range(2)]
+        xs = [[kept([P, 512], U8, f"xs{h}{c}") for c in range(CA + CB)] for h in range(2)]
+        prw = [[kept([P, 512], U32, f"prw{h}{g}") for g in range(2)] for h in range(2)]
+        prs = [[kept([P, 512], U8, f"prs{h}{g}") for g in range(2)] for h in range(2)]
+
+        ra_v = ra.rearrange("(h p b) k -> h p b k", h=2, p=P)
+        rb_v = rb.rearrange("(h p b) k -> h p b k", h=2, p=P)
+        y_v = y.rearrange("(h p b) v -> h p b v", h=2, p=P)
+        out_v = out.rearrange("(h p b) v -> h b p v", h=2, p=P)
+        pa_v = pa.rearrange("(c p j) f -> c p j f", c=CA, p=P)
+        pbw_v = pb_words.rearrange("g p n -> p g n")
+        pbs_v = pb_scales.rearrange("g r n -> r g n")
+        lw_v = load_words.rearrange("g p n -> p g n")
+        ls_v = load_scales.rearrange("g r n -> r g n")
+
+        def load_pb(g):
+            nc.sync.dma_start(
+                out=pb_raw[g][:].bitcast(I32), in_=pbw_v[:, :, 1024 * g : 1024 * (g + 1)].bitcast(I32)
+            )
+
+        def load_x(tiles, view, h, q):
+            nc.sync.dma_start(out=tiles[h][q][:], in_=view[h][:, 2 * q : 2 * q + 2, :])
+
+        def load_x1(tiles, view, h, b):
+            nc.sync.dma_start(out=tiles[h][b // 2][:, b % 2, :], in_=view[h][:, b, :])
+
+        def load_pa(g, c):
+            nc.sync.dma_start(out=pa_raw[g][c][:], in_=pa_v[c][:, :, 512 * g : 512 * (g + 1)])
+
+        nc.vector.memset(pbs_raw[:].bitcast(I32), 0)
+        nc.vector.memset(warm[:], 0.0)
+        make_identity(nc, ident[:])
+        for quad in range(4):
+            rows = slice(32 * quad, 32 * quad + 4)
+            nc.scalar.dma_start(out=pbs_raw[rows].bitcast(I32), in_=pbs_v[4 * quad : 4 * quad + 4].bitcast(I32))
+        nc.scalar.activation(out=warm[:], in_=warm[:], func=ACTF.Identity, bias=0.0, scale=1.0)
+        nc.vector.memset(ls[:].bitcast(I32), 0)
+        nc.gpsimd.dma_start(out=shrink_raw[:], in_=shrink.rearrange("(g p j) -> p g j", g=2, p=P))
+        nc.gpsimd.dma_start(out=prior_raw[:], in_=prior.rearrange("(g p j) -> p g j", g=2, p=P))
+        for quad in range(4):
+            rows = slice(32 * quad, 32 * quad + 4)
+            nc.gpsimd.dma_start(out=ls[rows].bitcast(I32), in_=ls_v[4 * quad : 4 * quad + 4].bitcast(I32))
+        load_x1(xb, rb_v, 0, 0)
+        load_x1(xb, rb_v, 0, 1)
+        load_pb(0)
+        load_x1(xb, rb_v, 0, 2)
+        load_x1(xb, rb_v, 0, 3)
+        load_pb(1)
+        for q in range(2):
+            load_x(xa, ra_v, 0, q)
+        for g in range(2):
+            for c in range(CA):
+                load_pa(g, c)
+        load_x1(ysb, y_v, 0, 0)
+        nc.sync.dma_start(out=lw[:].bitcast(I32), in_=lw_v.bitcast(I32))
+        nc.sync.dma_start(out=iv[:], in_=inv_vol.partition_broadcast(P))
+        for q in range(2):
+            load_x(xb, rb_v, 1, q)
+        load_x1(ysb, y_v, 0, 1)
+        for q in range(2):
+            load_x(xa, ra_v, 1, q)
+        load_x(ysb, y_v, 0, 1)
+        for q in range(2):
+            load_x(ysb, y_v, 1, q)
+
+        def move_pb_words(g, c):
+            nc.vector.tensor_copy(
+                out=pbw[g][c][:].rearrange("p (j m b) -> p j m b", j=4, b=2),
+                in_=pb_raw[g][:, c, :].rearrange("p (m j b) -> p j m b", j=4, b=2),
+            )
+
+        def move_pb_scales(g, c):
+            nc.vector.tensor_copy(
+                out=pbs[g][c][:].rearrange("p (j m) -> p j m", j=4),
+                in_=pbs_raw[:, c, 512 * g : 512 * (g + 1)].rearrange("p (m j) -> p j m", j=4),
+            )
+
+        sorted_words = {}
+
+        def sort_words(kind, q):
+            src = (xa if kind == "a" else xb)[1][q]
+            chunks = CA if kind == "a" else CB
+            t = kept([P, 2, chunks, 2, P], F32, f"x{kind}0{q}")
+            sorted_words[(kind, q)] = t
+            for blk in range(2):
+                nc.scalar.copy(
+                    out=t[:, blk],
+                    in_=src[:, blk, :].bitcast(F32).rearrange("p (c i u) -> p c u i", c=chunks, u=2),
+                )
+
+        grouped = {}
+        turned = {}
+
+        def turn(h, kind, c, q, b, blks=(0, 1)):
+            tiles = xa if kind == "a" else xb
+            if 0 in blks:
+                turned[(h, kind, c, q)] = bank(b)
+            pv = turned[(h, kind, c, q)][:].rearrange("p (u t) -> p u t", u=2)
+            for blk in blks:
+                for u in range(2):
+                    if h == 0:
+                        words = tiles[h][q][:, blk, :].bitcast(F32)[:, 256 * c + u : 256 * (c + 1) : 2]
+                    else:
+                        words = sorted_words[(kind, q)][:, blk, c, u, :]
+                    nc.tensor.transpose(pv[:, u, P * blk : P * (blk + 1)], words, ident[:])
+
+        def leave_turn(h, kind, c, q, engine):
+            key = (h, kind, c)
+            if key not in grouped:
+                grouped[key] = stage.tile([P, 512, 4], BF16, name="xg", tag="xg", bufs=4, align_bytes=64)
+            pv = turned[(h, kind, c, q)][:].rearrange("p (u t) -> p u t", u=2)
+            dst = grouped[key][:, 256 * q : 256 * (q + 1), :].bitcast(F32)
+            if engine == "act":
+                nc.scalar.copy(out=dst, in_=pv.rearrange("p u t -> p t u"))
+            else:
+                nc.vector.tensor_copy(out=dst, in_=pv.rearrange("p u t -> p t u"))
+
+        def quant_x(h, kind, c):
+            i = c if kind == "a" else CA + c
+            nc.vector.quantize_mx(
+                out=xw[h][i][:].bitcast(FP8X4),
+                scales=xs[h][i][:],
+                in_=grouped[(h, kind, c)][:].rearrange("p t j -> p (t j)"),
+            )
+
+        pa_grouped = {}
+
+        def group_pa(g, c):
+            t = stage.tile([P, 4, P, 4], BF16, name="pag", tag="pag", bufs=2, align_bytes=64)
+            pa_grouped[(g, c)] = t
+            src = pa_raw[g][c][:].rearrange("p k (m j) -> p j m k", j=4)
+            nc.scalar.copy(out=t[:, 2:], in_=src[:, 2:])
+            nc.vector.tensor_copy(out=t[:, :2], in_=src[:, :2])
+
+        def quant_pa(g, c):
+            nc.vector.quantize_mx(
+                out=paw[g][c][:].bitcast(FP8X4),
+                scales=pas[g][c][:],
+                in_=pa_grouped[(g, c)][:].rearrange("p j m k -> p (j m k)"),
+            )
+
+        order1 = list(range(CA, CA + CB)) + list(range(CA))
+
+        def pass1(out, h, g, j, i, cols=slice(0, 512)):
+            if i < CA:
+                lhs = paw[g][i][:, P * j : P * (j + 1)].bitcast(FP8X4)
+                lhs_scale = pas[g][i][:, P * j : P * (j + 1)]
+            else:
+                lhs = pbw[g][i - CA][:, 2 * P * j : 2 * P * (j + 1)].bitcast(FP4X4)
+                lhs_scale = pbs[g][i - CA][:, P * j : P * (j + 1)]
+            nc.tensor.matmul_mx(
+                out=out,
+                lhsT=lhs,
+                lhsT_scale=lhs_scale,
+                rhs=xw[h][i][:, cols].bitcast(FP8X4),
+                rhs_scale=xs[h][i][:, cols],
+                start=(i == order1[0]),
+                stop=(i == order1[-1]),
+            )
+
+        premia = {}
+
+        def leave1(ps, h, g, j, engine):
+            if (h, g) not in premia:
+                premia[(h, g)] = stage.tile([P, 4, 512], BF16, name="prem", tag="prem", bufs=2, align_bytes=64)
+            dst = premia[(h, g)][:, j, :]
+            if engine == "act":
+                nc.scalar.activation(
+                    out=dst, in_=ps[:], func=ACTF.Identity,
+                    bias=prior_f[:, g, j : j + 1], scale=shrink_f[:, g, j : j + 1],
+                )
+            else:
+                nc.vector.tensor_scalar(
+                    out=dst, in0=ps[:], scalar1=shrink_f[:, g, j : j + 1], scalar2=prior_f[:, g, j : j + 1],
+                    op0=ALU.mult, op1=ALU.add,
+                )
+
+        prem_grouped = {}
+
+        def group_premia(h, g, cut):
+            t = stage.tile([P, 512, 4], BF16, name="premg", tag="premg", bufs=2, align_bytes=64)
+            prem_grouped[(h, g)] = t
+            src = premia[(h, g)][:].rearrange("p j t -> p t j")
+            if cut < 512:
+                nc.scalar.copy(out=t[:, cut:, :], in_=src[:, cut:, :])
+            if cut > 0:
+                nc.vector.tensor_copy(out=t[:, :cut, :], in_=src[:, :cut, :])
+
+        def quant_premia(h, g):
+            nc.vector.quantize_mx(
+                out=prw[h][g][:].bitcast(FP8X4),
+                scales=prs[h][g][:],
+                in_=prem_grouped[(h, g)][:].rearrange("p t j -> p (t j)"),
+            )
+
+        block_premia = {}
+
+        def block_stage1(h, blk, b):
+            ps = bank(b)
+            pv = ps[:].rearrange("p (j t) -> p j t", j=4)
+            cols = slice(P * blk, P * (blk + 1))
+            for j in range(4):
+                for i in order1:
+                    pass1(pv[:, j, :], h, 1, j, i, cols)
+            t = stage.tile([P, 4, P], BF16, name="bprem", tag="bprem", bufs=3, align_bytes=64)
+            block_premia[(h, blk)] = t
+            for j in range(4):
+                nc.scalar.activation(
+                    out=t[:, j, :], in_=pv[:, j, :], func=ACTF.Identity,
+                    bias=prior_f[:, 1, j : j + 1], scale=shrink_f[:, 1, j : j + 1],
+                )
+
+        def block_group(h, blk, engine):
+            t = stage.tile([P, P, 4], BF16, name="bpremg", tag="bpremg", bufs=3, align_bytes=64)
+            src = block_premia[(h, blk)][:].rearrange("p j t -> p t j")
+            block_premia[(h, blk)] = t
+            if engine == "act":
+                nc.scalar.copy(out=t[:], in_=src)
+            else:
+                nc.vector.tensor_copy(out=t[:], in_=src)
+
+        def block_quant(h, blk):
+            cols = slice(P * blk, P * (blk + 1))
+            nc.vector.quantize_mx(
+                out=prw[h][1][:, cols].bitcast(FP8X4),
+                scales=prs[h][1][:, cols],
+                in_=block_premia[(h, blk)][:].rearrange("p t j -> p (t j)"),
+            )
+
+        results = {}
+        late = []
+
+        def stage2(h, unit, b):
+            blk, v = UNITS[unit]
+            ps = bank(b)
+            for g in range(2):
+                nc.tensor.matmul_mx(
+                    out=ps[:],
+                    lhsT=prw[h][g][:, P * blk : P * (blk + 1)].bitcast(FP8X4),
+                    lhsT_scale=prs[h][g][:, P * blk : P * (blk + 1)],
+                    rhs=lw[:, g, 1024 * v : 1024 * (v + 1)].bitcast(FP4X4),
+                    rhs_scale=ls[:, g, 512 * v : 512 * (v + 1)],
+                    start=(g == 0),
+                    stop=(g == 1),
+                )
+            key = (h, blk, v // 2)
+            if key not in results:
+                results[key] = stage.tile([P, 1024], F32, name="res", tag="res", bufs=5, align_bytes=64)
+            cols = slice(512 * (v % 2), 512 * (v % 2) + 512)
+            nc.vector.tensor_tensor(
+                out=results[key][:, cols], in0=ysb[h][blk // 2][:, blk % 2, 512 * v : 512 * (v + 1)],
+                in1=ps[:], op=ALU.subtract,
+            )
+            late.append((h, unit))
+            if len(late) > 1:
+                finish(late.pop(0))
+
+        def finish(item):
+            h, unit = item
+            blk, v = UNITS[unit]
+            key = (h, blk, v // 2)
+            cols = slice(512 * (v % 2), 512 * (v % 2) + 512)
+            eng = nc.vector if unit % B_ON_VECTOR == 1 else nc.gpsimd
+            eng.tensor_tensor(
+                out=results[key][:, cols], in0=results[key][:, cols], in1=iv[:, 512 * v : 512 * (v + 1)],
+                op=ALU.mult,
+            )
+            if v % 2 == 1:
+                nc.sync.dma_start(
+                    out=out_v[h, blk][:, 1024 * (v // 2) : 1024 * (v // 2 + 1)], in_=results[key][:]
+                )
+
+        for q in range(2):
+            for blk in range(2):
+                for c in range(CB):
+                    turn(0, "b", c, q, (4 if q == 0 else 0) + c, (blk,))
+            for c in range(CB):
+                leave_turn(0, "b", c, q, "act")
+        move_pb_words(0, 0)
+        move_pb_words(0, 1)
+        move_pb_scales(0, 0)
+        move_pb_words(0, 2)
+        quant_x(0, "b", 0)
+        move_pb_scales(0, 1)
+        quant_x(0, "b", 1)
+        move_pb_scales(0, 2)
+        quant_x(0, "b", 2)
+        quad = [bank(j) for j in range(4)]
+        for j in range(4):
+            pass1(quad[j][:], 0, 0, j, CA)
+        for q in range(2):
+            for c in range(CA):
+                turn(0, "a", c, q, 4 + 2 * q + c)
+                leave_turn(0, "a", c, q, "act")
+            for j in range(4):
+                pass1(quad[j][:], 0, 0, j, CA + 1 + q)
+        for c in range(CB):
+            move_pb_words(1, c)
+            move_pb_scales(1, c)
+        nc.vector.tensor_copy(out=shrink_f[:], in_=shrink_raw[:])
+        nc.vector.tensor_copy(out=prior_f[:], in_=prior_raw[:])
+        group_pa(0, 0)
+        quant_x(0, "a", 0)
+        quant_pa(0, 0)
+        group_pa(0, 1)
+        quant_x(0, "a", 1)
+        quant_pa(0, 1)
+        group_pa(1, 0)
+        group_pa(1, 1)
+        quant_pa(1, 0)
+        quant_pa(1, 1)
+        for j in range(4):
+            for i in range(CA):
+                pass1(quad[j][:], 0, 0, j, i)
+            leave1(quad[j], 0, 0, j, "act" if j % 2 == 0 else "dve")
+        group_premia(0, 0, 320)
+        block_stage1(0, 0, 4)
+        quant_premia(0, 0)
+        block_group(0, 0, "dve")
+        block_stage1(0, 1, 5)
+        block_quant(0, 0)
+        block_group(0, 1, "dve")
+        sort_words("b", 0)
+        block_quant(0, 1)
+
+        for unit in range(4):
+            stage2(0, unit, unit % 4)
+        block_stage1(0, 2, 6)
+        block_group(0, 2, "act")
+        for c in range(CB):
+            turn(1, "b", c, 0, (4, 5, 7)[c])
+            leave_turn(1, "b", c, 0, "act")
+        sort_words("b", 1)
+        block_stage1(0, 3, 6)
+        block_group(0, 3, "act")
+        for unit in range(4, 8):
+            if unit == 6:
+                block_quant(0, 2)
+            stage2(0, unit, unit % 4)
+        block_quant(0, 3)
+        for c in range(CB):
+            turn(1, "b", c, 1, (4, 5, 7)[c])
+            leave_turn(1, "b", c, 1, "dve" if c == 1 else "act")
+        for unit in range(8, 11):
+            stage2(0, unit, unit % 4)
+            quant_x(1, "b", unit - 8)
+        for q in range(2):
+            sort_words("a", q)
+        for q in range(2):
+            for c in range(CA):
+                turn(1, "a", c, q, 4 + 2 * q + c)
+                leave_turn(1, "a", c, q, "act" if c == 0 else "dve")
+        stage2(0, 11, 3)
+        quant_x(1, "a", 0)
+        quant_x(1, "a", 1)
+        for j in range(4):
+            ps = bank(4 + j)
+            for i in order1:
+                pass1(ps[:], 1, 0, j, i)
+            leave1(ps, 1, 0, j, "act")
+            if j > 0:
+                stage2(0, 11 + j, (11 + j) % 4)
+        group_premia(1, 0, 320)
+        block_stage1(1, 0, 4)
+        block_group(1, 0, "act")
+        stage2(0, 15, 3)
+        quant_premia(1, 0)
+        block_quant(1, 0)
+
+        for blk in range(4):
+            if blk < 3:
+                block_stage1(1, blk + 1, 5 + blk)
+                block_group(1, blk + 1, "act")
+            for v in range(4):
+                if v == 2 and blk < 3:
+                    block_quant(1, blk + 1)
+                stage2(1, 4 * blk + v, v)
+        finish(late.pop(0))

@@ -21,7 +21,10 @@ HALF = 512
 CA = NA // 512
 CB = NB // 512
 UNITS = [(b, v) for b in range(4) for v in range(4)]
-B_ON_VECTOR = 3
+ON_POOL = ()
+SORT = False
+PA_CUT = ((4, 2), (2, 2))
+LAG = 1
 
 
 def tile_cross_sectional_premia_residuals_s3_kernel(
@@ -88,12 +91,12 @@ def tile_cross_sectional_premia_residuals_s3_kernel(
         def load_pa(g, c):
             nc.sync.dma_start(out=pa_raw[g][c][:], in_=pa_v[c][:, :, 512 * g : 512 * (g + 1)])
 
-        nc.vector.memset(pbs_raw[:].bitcast(I32), 0)
         nc.vector.memset(warm[:], 0.0)
+        nc.vector.memset(pbs_raw[:].bitcast(I32), 0)
         make_identity(nc, ident[:])
         for quad in range(4):
             rows = slice(32 * quad, 32 * quad + 4)
-            nc.scalar.dma_start(out=pbs_raw[rows].bitcast(I32), in_=pbs_v[4 * quad : 4 * quad + 4].bitcast(I32))
+            nc.gpsimd.dma_start(out=pbs_raw[rows].bitcast(I32), in_=pbs_v[4 * quad : 4 * quad + 4].bitcast(I32))
         nc.scalar.activation(out=warm[:], in_=warm[:], func=ACTF.Identity, bias=0.0, scale=1.0)
         nc.vector.memset(ls[:].bitcast(I32), 0)
         nc.gpsimd.dma_start(out=shrink_raw[:], in_=shrink.rearrange("(g p j) -> p g j", g=2, p=P))
@@ -101,25 +104,23 @@ def tile_cross_sectional_premia_residuals_s3_kernel(
         for quad in range(4):
             rows = slice(32 * quad, 32 * quad + 4)
             nc.gpsimd.dma_start(out=ls[rows].bitcast(I32), in_=ls_v[4 * quad : 4 * quad + 4].bitcast(I32))
-        load_x1(xb, rb_v, 0, 0)
-        load_x1(xb, rb_v, 0, 1)
         load_pb(0)
-        load_x1(xb, rb_v, 0, 2)
-        load_x1(xb, rb_v, 0, 3)
+        for blk in range(4):
+            load_x1(xb, rb_v, 0, blk)
         load_pb(1)
         for q in range(2):
             load_x(xa, ra_v, 0, q)
         for g in range(2):
             for c in range(CA):
                 load_pa(g, c)
+        for q in range(2):
+            load_x(xb, rb_v, 1, q)
         load_x1(ysb, y_v, 0, 0)
         nc.sync.dma_start(out=lw[:].bitcast(I32), in_=lw_v.bitcast(I32))
         nc.sync.dma_start(out=iv[:], in_=inv_vol.partition_broadcast(P))
         for q in range(2):
-            load_x(xb, rb_v, 1, q)
-        load_x1(ysb, y_v, 0, 1)
-        for q in range(2):
             load_x(xa, ra_v, 1, q)
+        load_x1(ysb, y_v, 0, 1)
         load_x(ysb, y_v, 0, 1)
         for q in range(2):
             load_x(ysb, y_v, 1, q)
@@ -159,7 +160,7 @@ def tile_cross_sectional_premia_residuals_s3_kernel(
             pv = turned[(h, kind, c, q)][:].rearrange("p (u t) -> p u t", u=2)
             for blk in blks:
                 for u in range(2):
-                    if h == 0:
+                    if not (h == 1 and SORT):
                         words = tiles[h][q][:, blk, :].bitcast(F32)[:, 256 * c + u : 256 * (c + 1) : 2]
                     else:
                         words = sorted_words[(kind, q)][:, blk, c, u, :]
@@ -190,8 +191,10 @@ def tile_cross_sectional_premia_residuals_s3_kernel(
             t = stage.tile([P, 4, P, 4], BF16, name="pag", tag="pag", bufs=2, align_bytes=64)
             pa_grouped[(g, c)] = t
             src = pa_raw[g][c][:].rearrange("p k (m j) -> p j m k", j=4)
-            nc.scalar.copy(out=t[:, 2:], in_=src[:, 2:])
-            nc.vector.tensor_copy(out=t[:, :2], in_=src[:, :2])
+            cut = PA_CUT[g][c]
+            nc.vector.tensor_copy(out=t[:, :cut], in_=src[:, :cut])
+            if cut < 4:
+                nc.scalar.copy(out=t[:, cut:], in_=src[:, cut:])
 
         def quant_pa(g, c):
             nc.vector.quantize_mx(
@@ -313,7 +316,7 @@ def tile_cross_sectional_premia_residuals_s3_kernel(
                 in1=ps[:], op=ALU.subtract,
             )
             late.append((h, unit))
-            if len(late) > 1:
+            if len(late) > LAG:
                 finish(late.pop(0))
 
         def finish(item):
@@ -321,7 +324,7 @@ def tile_cross_sectional_premia_residuals_s3_kernel(
             blk, v = UNITS[unit]
             key = (h, blk, v // 2)
             cols = slice(512 * (v % 2), 512 * (v % 2) + 512)
-            eng = nc.vector if unit % B_ON_VECTOR == 1 else nc.gpsimd
+            eng = nc.gpsimd if v in ON_POOL else nc.vector
             eng.tensor_tensor(
                 out=results[key][:, cols], in0=results[key][:, cols], in1=iv[:, 512 * v : 512 * (v + 1)],
                 op=ALU.mult,
@@ -331,109 +334,124 @@ def tile_cross_sectional_premia_residuals_s3_kernel(
                     out=out_v[h, blk][:, 1024 * (v // 2) : 1024 * (v // 2 + 1)], in_=results[key][:]
                 )
 
+        move_pb_words(0, 0)
+        move_pb_words(0, 1)
+        move_pb_words(0, 2)
         for q in range(2):
             for blk in range(2):
                 for c in range(CB):
                     turn(0, "b", c, q, (4 if q == 0 else 0) + c, (blk,))
             for c in range(CB):
-                leave_turn(0, "b", c, q, "act")
-        move_pb_words(0, 0)
-        move_pb_words(0, 1)
-        move_pb_scales(0, 0)
-        move_pb_words(0, 2)
+                leave_turn(0, "b", c, q, "dve" if (q == 1 and c == 1) else "act")
         quant_x(0, "b", 0)
-        move_pb_scales(0, 1)
+        move_pb_scales(0, 0)
         quant_x(0, "b", 1)
-        move_pb_scales(0, 2)
+        move_pb_scales(0, 1)
         quant_x(0, "b", 2)
+        move_pb_scales(0, 2)
         quad = [bank(j) for j in range(4)]
         for j in range(4):
             pass1(quad[j][:], 0, 0, j, CA)
-        for q in range(2):
-            for c in range(CA):
-                turn(0, "a", c, q, 4 + 2 * q + c)
-                leave_turn(0, "a", c, q, "act")
-            for j in range(4):
-                pass1(quad[j][:], 0, 0, j, CA + 1 + q)
-        for c in range(CB):
-            move_pb_words(1, c)
-            move_pb_scales(1, c)
-        nc.vector.tensor_copy(out=shrink_f[:], in_=shrink_raw[:])
-        nc.vector.tensor_copy(out=prior_f[:], in_=prior_raw[:])
+        for c in range(CA):
+            turn(0, "a", c, 0, 4 + c)
+            leave_turn(0, "a", c, 0, "act")
+        move_pb_words(1, 0)
         group_pa(0, 0)
-        quant_x(0, "a", 0)
+        for j in range(4):
+            pass1(quad[j][:], 0, 0, j, CA + 1)
+        for c in range(CA):
+            turn(0, "a", c, 1, 6 + c)
+            leave_turn(0, "a", c, 1, "act")
+        for j in range(4):
+            pass1(quad[j][:], 0, 0, j, CA + 2)
         quant_pa(0, 0)
         group_pa(0, 1)
+        move_pb_words(1, 1)
+        quant_x(0, "a", 0)
         quant_x(0, "a", 1)
         quant_pa(0, 1)
+        move_pb_words(1, 2)
         group_pa(1, 0)
-        group_pa(1, 1)
+        nc.vector.tensor_copy(out=shrink_f[:], in_=shrink_raw[:])
+        nc.vector.tensor_copy(out=prior_f[:], in_=prior_raw[:])
+        move_pb_scales(1, 0)
         quant_pa(1, 0)
+        move_pb_scales(1, 1)
+        group_pa(1, 1)
+        move_pb_scales(1, 2)
         quant_pa(1, 1)
         for j in range(4):
             for i in range(CA):
                 pass1(quad[j][:], 0, 0, j, i)
-            leave1(quad[j], 0, 0, j, "act" if j % 2 == 0 else "dve")
-        group_premia(0, 0, 320)
+            leave1(quad[j], 0, 0, j, "act")
+
+        def turns(kind, q, banks):
+            for c in range(CB if kind == "b" else CA):
+                turn(1, kind, c, q, banks[c])
+                leave_turn(1, kind, c, q, "act")
+
+        def units(h, first, last):
+            for unit in range(first, last):
+                stage2(h, unit, unit % 4)
+
+        turns("b", 0, (5, 6, 7))
         block_stage1(0, 0, 4)
-        quant_premia(0, 0)
+        group_premia(0, 0, 320)
         block_group(0, 0, "dve")
+        quant_premia(0, 0)
         block_stage1(0, 1, 5)
         block_quant(0, 0)
-        block_group(0, 1, "dve")
-        sort_words("b", 0)
+        block_group(0, 1, "act")
+        turns("b", 1, (6, 7, 4))
+        units(0, 0, 2)
         block_quant(0, 1)
-
-        for unit in range(4):
-            stage2(0, unit, unit % 4)
-        block_stage1(0, 2, 6)
+        units(0, 2, 4)
+        quant_x(1, "b", 0)
+        block_stage1(0, 2, 5)
         block_group(0, 2, "act")
-        for c in range(CB):
-            turn(1, "b", c, 0, (4, 5, 7)[c])
-            leave_turn(1, "b", c, 0, "act")
-        sort_words("b", 1)
+        units(0, 4, 5)
+        quant_x(1, "b", 1)
+        units(0, 5, 6)
+        quant_x(1, "b", 2)
+        turns("a", 0, (6, 7))
+        turns("a", 1, (4, 5))
+        block_quant(0, 2)
         block_stage1(0, 3, 6)
         block_group(0, 3, "act")
-        for unit in range(4, 8):
-            if unit == 6:
-                block_quant(0, 2)
-            stage2(0, unit, unit % 4)
-        block_quant(0, 3)
-        for c in range(CB):
-            turn(1, "b", c, 1, (4, 5, 7)[c])
-            leave_turn(1, "b", c, 1, "dve" if c == 1 else "act")
-        for unit in range(8, 11):
-            stage2(0, unit, unit % 4)
-            quant_x(1, "b", unit - 8)
-        for q in range(2):
-            sort_words("a", q)
-        for q in range(2):
-            for c in range(CA):
-                turn(1, "a", c, q, 4 + 2 * q + c)
-                leave_turn(1, "a", c, q, "act" if c == 0 else "dve")
-        stage2(0, 11, 3)
+        units(0, 6, 7)
         quant_x(1, "a", 0)
+        units(0, 7, 8)
         quant_x(1, "a", 1)
+        block_quant(0, 3)
+        units(0, 8, 9)
         for j in range(4):
-            ps = bank(4 + j)
-            for i in order1:
+            ps = bank((7, 4, 5, 6)[j])
+            for i in order1[:3]:
+                pass1(ps[:], 1, 0, j, i)
+            units(0, 9 + j, 10 + j)
+            for i in order1[3:]:
                 pass1(ps[:], 1, 0, j, i)
             leave1(ps, 1, 0, j, "act")
-            if j > 0:
-                stage2(0, 11 + j, (11 + j) % 4)
-        group_premia(1, 0, 320)
-        block_stage1(1, 0, 4)
+        group_premia(1, 0, 0)
+        block_stage1(1, 0, 7)
         block_group(1, 0, "act")
-        stage2(0, 15, 3)
+        units(0, 13, 14)
+        block_stage1(1, 1, 4)
+        block_group(1, 1, "act")
+        units(0, 14, 15)
         quant_premia(1, 0)
         block_quant(1, 0)
-
-        for blk in range(4):
-            if blk < 3:
-                block_stage1(1, blk + 1, 5 + blk)
-                block_group(1, blk + 1, "act")
-            for v in range(4):
-                if v == 2 and blk < 3:
-                    block_quant(1, blk + 1)
-                stage2(1, 4 * blk + v, v)
-        finish(late.pop(0))
+        units(0, 15, 16)
+        units(1, 0, 2)
+        block_stage1(1, 2, 5)
+        block_group(1, 2, "act")
+        block_quant(1, 1)
+        units(1, 2, 5)
+        block_stage1(1, 3, 6)
+        block_group(1, 3, "act")
+        block_quant(1, 2)
+        units(1, 5, 8)
+        block_quant(1, 3)
+        units(1, 8, 16)
+        while late:
+            finish(late.pop(0))

from contextlib import ExitStack

import concourse.mybir as mybir
from concourse.masks import make_identity

F32 = mybir.dt.float32
BF16 = mybir.dt.bfloat16
I32 = mybir.dt.int32
U32 = mybir.dt.uint32
U8 = mybir.dt.uint8
FP8X4 = mybir.dt.float8_e4m3fn_x4
FP4X4 = mybir.dt.float4_e2m1fn_x4
ALU = mybir.AluOpType
ACTF = mybir.ActivationFunctionType

P = 128
T, NA, NB, F, V = 1024, 1024, 1536, 1024, 2048
FLOPS = 2 * T * F * (NA + NB) + 2 * T * F * V

HALF = 512
CA = NA // 512
CB = NB // 512
UNITS = [(b, v) for b in range(4) for v in range(4)]
ON_POOL = ()
SORT = False
PA_CUT = ((4, 2), (2, 2))
LAG = 1


def tile_cross_sectional_premia_residuals_s3_kernel(
    tc, ra, pa, rb, pb_words, pb_scales, shrink, prior, load_words, load_scales, y, inv_vol, out
):
    nc = tc.nc
    with ExitStack() as ctx:
        keep = ctx.enter_context(tc.tile_pool(name="keep", bufs=1))
        stage = ctx.enter_context(tc.tile_pool(name="stage", bufs=2))
        psum = ctx.enter_context(tc.psum_pool(name="psum", bufs=1))
        ctx.enter_context(tc.manual_schedule())

        def bank(i):
            return psum.tile([P, 512], F32, name=f"bank{i}", tag=f"bank{i}", bufs=1)

        def kept(shape, dtype, name):
            return keep.tile(shape, dtype, name=name, tag=name, align_bytes=64)

        ident = kept([P, P], F32, "ident")
        pb_raw = [kept([P, CB, 1024], U8, f"pb_raw{g}") for g in range(2)]
        pbs_raw = kept([P, CB, F], U8, "pbs_raw")
        pbw = [[kept([P, 1024], U8, f"pbw{g}_{c}") for c in range(CB)] for g in range(2)]
        pbs = [[kept([P, 512], U8, f"pbs{g}_{c}") for c in range(CB)] for g in range(2)]
        lw = kept([P, 2, 2 * V], U8, "lw")
        ls = kept([P, 2, V], U8, "ls")
        shrink_raw = kept([P, 2, 4], BF16, "shrink_raw")
        prior_raw = kept([P, 2, 4], BF16, "prior_raw")
        shrink_f = kept([P, 2, 4], F32, "shrink_f")
        prior_f = kept([P, 2, 4], F32, "prior_f")
        warm = kept([P, 1], F32, "warm")
        iv = kept([P, V], BF16, "iv")
        xa = [[kept([P, 2, NA], BF16, f"xa{h}{q}") for q in range(2)] for h in range(2)]
        xb = [[kept([P, 2, NB], BF16, f"xb{h}{q}") for q in range(2)] for h in range(2)]
        pa_raw = [[kept([P, 4, 512], BF16, f"pa_raw{g}{c}") for c in range(CA)] for g in range(2)]
        ysb = [[kept([P, 2, V], BF16, f"y{h}{q}") for q in range(2)] for h in range(2)]
        paw = [[kept([P, 512], U32, f"paw{g}{c}") for c in range(CA)] for g in range(2)]
        pas = [[kept([P, 512], U8, f"pas{g}{c}") for c in range(CA)] for g in range(2)]
        xw = [[kept([P, 512], U32, f"xw{h}{c}") for c in range(CA + CB)] for h in range(2)]
        xs = [[kept([P, 512], U8, f"xs{h}{c}") for c in range(CA + CB)] for h in range(2)]
        prw = [[kept([P, 512], U32, f"prw{h}{g}") for g in range(2)] for h in range(2)]
        prs = [[kept([P, 512], U8, f"prs{h}{g}") for g in range(2)] for h in range(2)]

        ra_v = ra.rearrange("(h p b) k -> h p b k", h=2, p=P)
        rb_v = rb.rearrange("(h p b) k -> h p b k", h=2, p=P)
        y_v = y.rearrange("(h p b) v -> h p b v", h=2, p=P)
        out_v = out.rearrange("(h p b) v -> h b p v", h=2, p=P)
        pa_v = pa.rearrange("(c p j) f -> c p j f", c=CA, p=P)
        pbw_v = pb_words.rearrange("g p n -> p g n")
        pbs_v = pb_scales.rearrange("g r n -> r g n")
        lw_v = load_words.rearrange("g p n -> p g n")
        ls_v = load_scales.rearrange("g r n -> r g n")

        def load_pb(g):
            nc.sync.dma_start(
                out=pb_raw[g][:].bitcast(I32), in_=pbw_v[:, :, 1024 * g : 1024 * (g + 1)].bitcast(I32)
            )

        def load_x(tiles, view, h, q):
            nc.sync.dma_start(out=tiles[h][q][:], in_=view[h][:, 2 * q : 2 * q + 2, :])

        def load_x1(tiles, view, h, b):
            nc.sync.dma_start(out=tiles[h][b // 2][:, b % 2, :], in_=view[h][:, b, :])

        def load_pa(g, c):
            nc.sync.dma_start(out=pa_raw[g][c][:], in_=pa_v[c][:, :, 512 * g : 512 * (g + 1)])

        nc.vector.memset(warm[:], 0.0)
        nc.vector.memset(pbs_raw[:].bitcast(I32), 0)
        make_identity(nc, ident[:])
        for quad in range(4):
            rows = slice(32 * quad, 32 * quad + 4)
            nc.gpsimd.dma_start(out=pbs_raw[rows].bitcast(I32), in_=pbs_v[4 * quad : 4 * quad + 4].bitcast(I32))
        nc.scalar.activation(out=warm[:], in_=warm[:], func=ACTF.Identity, bias=0.0, scale=1.0)
        nc.vector.memset(ls[:].bitcast(I32), 0)
        nc.gpsimd.dma_start(out=shrink_raw[:], in_=shrink.rearrange("(g p j) -> p g j", g=2, p=P))
        nc.gpsimd.dma_start(out=prior_raw[:], in_=prior.rearrange("(g p j) -> p g j", g=2, p=P))
        for quad in range(4):
            rows = slice(32 * quad, 32 * quad + 4)
            nc.gpsimd.dma_start(out=ls[rows].bitcast(I32), in_=ls_v[4 * quad : 4 * quad + 4].bitcast(I32))
        load_pb(0)
        for blk in range(4):
            load_x1(xb, rb_v, 0, blk)
        load_pb(1)
        for q in range(2):
            load_x(xa, ra_v, 0, q)
        for g in range(2):
            for c in range(CA):
                load_pa(g, c)
        for q in range(2):
            load_x(xb, rb_v, 1, q)
        load_x1(ysb, y_v, 0, 0)
        nc.sync.dma_start(out=lw[:].bitcast(I32), in_=lw_v.bitcast(I32))
        nc.sync.dma_start(out=iv[:], in_=inv_vol.partition_broadcast(P))
        for q in range(2):
            load_x(xa, ra_v, 1, q)
        load_x1(ysb, y_v, 0, 1)
        load_x(ysb, y_v, 0, 1)
        for q in range(2):
            load_x(ysb, y_v, 1, q)

        def move_pb_words(g, c):
            nc.vector.tensor_copy(
                out=pbw[g][c][:].rearrange("p (j m b) -> p j m b", j=4, b=2),
                in_=pb_raw[g][:, c, :].rearrange("p (m j b) -> p j m b", j=4, b=2),
            )

        def move_pb_scales(g, c):
            nc.vector.tensor_copy(
                out=pbs[g][c][:].rearrange("p (j m) -> p j m", j=4),
                in_=pbs_raw[:, c, 512 * g : 512 * (g + 1)].rearrange("p (m j) -> p j m", j=4),
            )

        sorted_words = {}

        def sort_words(kind, q):
            src = (xa if kind == "a" else xb)[1][q]
            chunks = CA if kind == "a" else CB
            t = kept([P, 2, chunks, 2, P], F32, f"x{kind}0{q}")
            sorted_words[(kind, q)] = t
            for blk in range(2):
                nc.scalar.copy(
                    out=t[:, blk],
                    in_=src[:, blk, :].bitcast(F32).rearrange("p (c i u) -> p c u i", c=chunks, u=2),
                )

        grouped = {}
        turned = {}

        def turn(h, kind, c, q, b, blks=(0, 1)):
            tiles = xa if kind == "a" else xb
            if 0 in blks:
                turned[(h, kind, c, q)] = bank(b)
            pv = turned[(h, kind, c, q)][:].rearrange("p (u t) -> p u t", u=2)
            for blk in blks:
                for u in range(2):
                    if not (h == 1 and SORT):
                        words = tiles[h][q][:, blk, :].bitcast(F32)[:, 256 * c + u : 256 * (c + 1) : 2]
                    else:
                        words = sorted_words[(kind, q)][:, blk, c, u, :]
                    nc.tensor.transpose(pv[:, u, P * blk : P * (blk + 1)], words, ident[:])

        def leave_turn(h, kind, c, q, engine):
            key = (h, kind, c)
            if key not in grouped:
                grouped[key] = stage.tile([P, 512, 4], BF16, name="xg", tag="xg", bufs=4, align_bytes=64)
            pv = turned[(h, kind, c, q)][:].rearrange("p (u t) -> p u t", u=2)
            dst = grouped[key][:, 256 * q : 256 * (q + 1), :].bitcast(F32)
            if engine == "act":
                nc.scalar.copy(out=dst, in_=pv.rearrange("p u t -> p t u"))
            else:
                nc.vector.tensor_copy(out=dst, in_=pv.rearrange("p u t -> p t u"))

        def quant_x(h, kind, c):
            i = c if kind == "a" else CA + c
            nc.vector.quantize_mx(
                out=xw[h][i][:].bitcast(FP8X4),
                scales=xs[h][i][:],
                in_=grouped[(h, kind, c)][:].rearrange("p t j -> p (t j)"),
            )

        pa_grouped = {}

        def group_pa(g, c):
            t = stage.tile([P, 4, P, 4], BF16, name="pag", tag="pag", bufs=2, align_bytes=64)
            pa_grouped[(g, c)] = t
            src = pa_raw[g][c][:].rearrange("p k (m j) -> p j m k", j=4)
            cut = PA_CUT[g][c]
            nc.vector.tensor_copy(out=t[:, :cut], in_=src[:, :cut])
            if cut < 4:
                nc.scalar.copy(out=t[:, cut:], in_=src[:, cut:])

        def quant_pa(g, c):
            nc.vector.quantize_mx(
                out=paw[g][c][:].bitcast(FP8X4),
                scales=pas[g][c][:],
                in_=pa_grouped[(g, c)][:].rearrange("p j m k -> p (j m k)"),
            )

        order1 = list(range(CA, CA + CB)) + list(range(CA))

        def pass1(out, h, g, j, i, cols=slice(0, 512)):
            if i < CA:
                lhs = paw[g][i][:, P * j : P * (j + 1)].bitcast(FP8X4)
                lhs_scale = pas[g][i][:, P * j : P * (j + 1)]
            else:
                lhs = pbw[g][i - CA][:, 2 * P * j : 2 * P * (j + 1)].bitcast(FP4X4)
                lhs_scale = pbs[g][i - CA][:, P * j : P * (j + 1)]
            nc.tensor.matmul_mx(
                out=out,
                lhsT=lhs,
                lhsT_scale=lhs_scale,
                rhs=xw[h][i][:, cols].bitcast(FP8X4),
                rhs_scale=xs[h][i][:, cols],
                start=(i == order1[0]),
                stop=(i == order1[-1]),
            )

        premia = {}

        def leave1(ps, h, g, j, engine):
            if (h, g) not in premia:
                premia[(h, g)] = stage.tile([P, 4, 512], BF16, name="prem", tag="prem", bufs=2, align_bytes=64)
            dst = premia[(h, g)][:, j, :]
            if engine == "act":
                nc.scalar.activation(
                    out=dst, in_=ps[:], func=ACTF.Identity,
                    bias=prior_f[:, g, j : j + 1], scale=shrink_f[:, g, j : j + 1],
                )
            else:
                nc.vector.tensor_scalar(
                    out=dst, in0=ps[:], scalar1=shrink_f[:, g, j : j + 1], scalar2=prior_f[:, g, j : j + 1],
                    op0=ALU.mult, op1=ALU.add,
                )

        prem_grouped = {}

        def group_premia(h, g, cut):
            t = stage.tile([P, 512, 4], BF16, name="premg", tag="premg", bufs=2, align_bytes=64)
            prem_grouped[(h, g)] = t
            src = premia[(h, g)][:].rearrange("p j t -> p t j")
            if cut < 512:
                nc.scalar.copy(out=t[:, cut:, :], in_=src[:, cut:, :])
            if cut > 0:
                nc.vector.tensor_copy(out=t[:, :cut, :], in_=src[:, :cut, :])

        def quant_premia(h, g):
            nc.vector.quantize_mx(
                out=prw[h][g][:].bitcast(FP8X4),
                scales=prs[h][g][:],
                in_=prem_grouped[(h, g)][:].rearrange("p t j -> p (t j)"),
            )

        block_premia = {}

        def block_stage1(h, blk, b):
            ps = bank(b)
            pv = ps[:].rearrange("p (j t) -> p j t", j=4)
            cols = slice(P * blk, P * (blk + 1))
            for j in range(4):
                for i in order1:
                    pass1(pv[:, j, :], h, 1, j, i, cols)
            t = stage.tile([P, 4, P], BF16, name="bprem", tag="bprem", bufs=3, align_bytes=64)
            block_premia[(h, blk)] = t
            for j in range(4):
                nc.scalar.activation(
                    out=t[:, j, :], in_=pv[:, j, :], func=ACTF.Identity,
                    bias=prior_f[:, 1, j : j + 1], scale=shrink_f[:, 1, j : j + 1],
                )

        def block_group(h, blk, engine):
            t = stage.tile([P, P, 4], BF16, name="bpremg", tag="bpremg", bufs=3, align_bytes=64)
            src = block_premia[(h, blk)][:].rearrange("p j t -> p t j")
            block_premia[(h, blk)] = t
            if engine == "act":
                nc.scalar.copy(out=t[:], in_=src)
            else:
                nc.vector.tensor_copy(out=t[:], in_=src)

        def block_quant(h, blk):
            cols = slice(P * blk, P * (blk + 1))
            nc.vector.quantize_mx(
                out=prw[h][1][:, cols].bitcast(FP8X4),
                scales=prs[h][1][:, cols],
                in_=block_premia[(h, blk)][:].rearrange("p t j -> p (t j)"),
            )

        results = {}
        late = []

        def stage2(h, unit, b):
            blk, v = UNITS[unit]
            ps = bank(b)
            for g in range(2):
                nc.tensor.matmul_mx(
                    out=ps[:],
                    lhsT=prw[h][g][:, P * blk : P * (blk + 1)].bitcast(FP8X4),
                    lhsT_scale=prs[h][g][:, P * blk : P * (blk + 1)],
                    rhs=lw[:, g, 1024 * v : 1024 * (v + 1)].bitcast(FP4X4),
                    rhs_scale=ls[:, g, 512 * v : 512 * (v + 1)],
                    start=(g == 0),
                    stop=(g == 1),
                )
            key = (h, blk, v // 2)
            if key not in results:
                results[key] = stage.tile([P, 1024], F32, name="res", tag="res", bufs=5, align_bytes=64)
            cols = slice(512 * (v % 2), 512 * (v % 2) + 512)
            nc.vector.tensor_tensor(
                out=results[key][:, cols], in0=ysb[h][blk // 2][:, blk % 2, 512 * v : 512 * (v + 1)],
                in1=ps[:], op=ALU.subtract,
            )
            late.append((h, unit))
            if len(late) > LAG:
                finish(late.pop(0))

        def finish(item):
            h, unit = item
            blk, v = UNITS[unit]
            key = (h, blk, v // 2)
            cols = slice(512 * (v % 2), 512 * (v % 2) + 512)
            eng = nc.gpsimd if v in ON_POOL else nc.vector
            eng.tensor_tensor(
                out=results[key][:, cols], in0=results[key][:, cols], in1=iv[:, 512 * v : 512 * (v + 1)],
                op=ALU.mult,
            )
            if v % 2 == 1:
                nc.sync.dma_start(
                    out=out_v[h, blk][:, 1024 * (v // 2) : 1024 * (v // 2 + 1)], in_=results[key][:]
                )

        move_pb_words(0, 0)
        move_pb_words(0, 1)
        move_pb_words(0, 2)
        for q in range(2):
            for blk in range(2):
                for c in range(CB):
                    turn(0, "b", c, q, (4 if q == 0 else 0) + c, (blk,))
            for c in range(CB):
                leave_turn(0, "b", c, q, "dve" if (q == 1 and c == 1) else "act")
        quant_x(0, "b", 0)
        move_pb_scales(0, 0)
        quant_x(0, "b", 1)
        move_pb_scales(0, 1)
        quant_x(0, "b", 2)
        move_pb_scales(0, 2)
        quad = [bank(j) for j in range(4)]
        for j in range(4):
            pass1(quad[j][:], 0, 0, j, CA)
        for c in range(CA):
            turn(0, "a", c, 0, 4 + c)
            leave_turn(0, "a", c, 0, "act")
        move_pb_words(1, 0)
        group_pa(0, 0)
        for j in range(4):
            pass1(quad[j][:], 0, 0, j, CA + 1)
        for c in range(CA):
            turn(0, "a", c, 1, 6 + c)
            leave_turn(0, "a", c, 1, "act")
        for j in range(4):
            pass1(quad[j][:], 0, 0, j, CA + 2)
        quant_pa(0, 0)
        group_pa(0, 1)
        move_pb_words(1, 1)
        quant_x(0, "a", 0)
        quant_x(0, "a", 1)
        quant_pa(0, 1)
        move_pb_words(1, 2)
        group_pa(1, 0)
        nc.vector.tensor_copy(out=shrink_f[:], in_=shrink_raw[:])
        nc.vector.tensor_copy(out=prior_f[:], in_=prior_raw[:])
        move_pb_scales(1, 0)
        quant_pa(1, 0)
        move_pb_scales(1, 1)
        group_pa(1, 1)
        move_pb_scales(1, 2)
        quant_pa(1, 1)
        for j in range(4):
            for i in range(CA):
                pass1(quad[j][:], 0, 0, j, i)
            leave1(quad[j], 0, 0, j, "act")

        def turns(kind, q, banks):
            for c in range(CB if kind == "b" else CA):
                turn(1, kind, c, q, banks[c])
                leave_turn(1, kind, c, q, "act")

        def units(h, first, last):
            for unit in range(first, last):
                stage2(h, unit, unit % 4)

        turns("b", 0, (5, 6, 7))
        block_stage1(0, 0, 4)
        group_premia(0, 0, 320)
        block_group(0, 0, "dve")
        quant_premia(0, 0)
        block_stage1(0, 1, 5)
        block_quant(0, 0)
        block_group(0, 1, "act")
        turns("b", 1, (6, 7, 4))
        units(0, 0, 2)
        block_quant(0, 1)
        units(0, 2, 4)
        quant_x(1, "b", 0)
        block_stage1(0, 2, 5)
        block_group(0, 2, "act")
        units(0, 4, 5)
        quant_x(1, "b", 1)
        units(0, 5, 6)
        quant_x(1, "b", 2)
        turns("a", 0, (6, 7))
        turns("a", 1, (4, 5))
        block_quant(0, 2)
        block_stage1(0, 3, 6)
        block_group(0, 3, "act")
        units(0, 6, 7)
        quant_x(1, "a", 0)
        units(0, 7, 8)
        quant_x(1, "a", 1)
        block_quant(0, 3)
        units(0, 8, 9)
        for j in range(4):
            ps = bank((7, 4, 5, 6)[j])
            for i in order1[:3]:
                pass1(ps[:], 1, 0, j, i)
            units(0, 9 + j, 10 + j)
            for i in order1[3:]:
                pass1(ps[:], 1, 0, j, i)
            leave1(ps, 1, 0, j, "act")
        group_premia(1, 0, 0)
        block_stage1(1, 0, 7)
        block_group(1, 0, "act")
        units(0, 13, 14)
        block_stage1(1, 1, 4)
        block_group(1, 1, "act")
        units(0, 14, 15)
        quant_premia(1, 0)
        block_quant(1, 0)
        units(0, 15, 16)
        units(1, 0, 2)
        block_stage1(1, 2, 5)
        block_group(1, 2, "act")
        block_quant(1, 1)
        units(1, 2, 5)
        block_stage1(1, 3, 6)
        block_group(1, 3, "act")
        block_quant(1, 2)
        units(1, 5, 8)
        block_quant(1, 3)
        units(1, 8, 16)
        while late:
            finish(late.pop(0))
